import numpy as np
import ml_dtypes


def mxq(x, axis, fmt="e4m3"):
    dtype, down = {"e4m3": (ml_dtypes.float8_e4m3fn, 7), "e5m2": (ml_dtypes.float8_e5m2, 14)}[fmt]
    v = np.moveaxis(np.asarray(x, np.float32).astype(ml_dtypes.bfloat16).astype(np.float64), axis, -1)
    blocks = v.reshape(v.shape[:-1] + (-1, 32))
    amax = np.abs(blocks).max(-1, keepdims=True)
    byte = np.maximum(np.where(amax > 0, np.frexp(amax)[1] - 1 + 127, 0) - down, 1)
    scale = np.exp2(byte - 127.0)
    codes = (blocks / scale).astype(np.float32).astype(dtype).astype(np.float64)
    return np.moveaxis((codes * scale).reshape(v.shape), -1, axis)


WIDE = False


def mx_kscale(k):
    if not WIDE:
        return np.ones(k)
    levels = np.array([10, -10, 5, -5, 0])
    if k % 512:
        return np.exp2(np.random.permutation(np.resize(levels, k // 32))).repeat(32)
    a = np.empty((k // 512, 16))
    for p in range(k // 512):
        a[p, :8] = np.random.permutation(np.resize(levels, 8))
        for g in range(8):
            far = levels[np.abs(levels - a[p, g]) >= 10]
            a[p, g + 8] = far[np.random.randint(len(far))]
    return np.exp2(a.ravel()).repeat(32)


def f64(x):
    return np.asarray(x).astype(np.float64)


def striped(idx):
    return np.tile(idx.reshape(-1, 16).T, (8, 1)).astype(np.uint16)


def unstriped(offs):
    return offs[:16].T.reshape(-1).astype(np.int64)


def gelu(v):
    return 0.5 * v * (1.0 + np.tanh(np.sqrt(2.0 / np.pi) * (v + 0.044715 * v**3)))


K, T, E, C, H, N = 1536, 512, 4, 256, 512, 128


def by_expert(wq, xq):
    return np.concatenate([wq[e].T @ xq[:, e * C:(e + 1) * C] for e in range(E)], axis=1)


def setup_inputs():
    n = np.random.standard_normal
    s = mx_kscale(K)[:, None]
    u = mx_kscale(H)
    first = np.random.permutation(np.repeat(np.arange(E), T // E))
    second = (first + 1 + np.random.permutation(np.repeat(np.arange(E - 1), -(-T // (E - 1)))[:T])) % E
    while np.bincount(second, minlength=E).max() != T // E:
        load = np.bincount(second, minlength=E); hi, lo = int(load.argmax()), int(load.argmin())
        t = np.flatnonzero((second == hi) & (first != lo))[0]; second[t] = lo
    slot_token = np.empty(E * C, np.int64); pos = np.empty((2, T), np.int64); fill = np.zeros(E, np.int64)
    place = np.stack([np.random.permutation(C) for _ in range(E)])
    for r, deal in enumerate((first, second)):
        for t in np.random.permutation(T):
            e = deal[t]; j = e * C + place[e, fill[e]]; fill[e] += 1; slot_token[j] = t; pos[r, t] = j
    g = np.random.uniform(0.2, 0.8, T)
    return {
        "xT": (n((K, T)) * s).astype(np.float32),
        "w1": (n((E, K, H)) / np.sqrt(K) / s[None] * u[None, None, :]).astype(np.float32),
        "w2": (n((E, H, N)) / np.sqrt(H) / u[None, :, None]).astype(np.float32),
        "gate": np.stack([np.tile(g, (N, 1)), np.tile(1.0 - g, (N, 1))]).astype(np.float32),
        "offs": striped(slot_token),
        "pos1": striped(pos[0]),
        "pos2": striped(pos[1]),
    }


def reference(xT, w1, w2, gate, offs, pos1, pos2):
    idx = unstriped(offs)
    xq = mxq(f64(xT)[:, idx], 0, "e4m3")
    h = gelu(by_expert(mxq(f64(w1), 1, "e4m3"), xq))
    y = by_expert(mxq(f64(w2), 1, "e4m3"), mxq(h, 0, "e4m3"))
    return f64(gate[0]) * y[:, unstriped(pos1)] + f64(gate[1]) * y[:, unstriped(pos2)]

@@ -1,0 +1,303 @@
+from contextlib import ExitStack
+
+import concourse.mybir as mybir
+
+K, T, E, C, H, N = 1536, 512, 4, 256, 512, 128
+FLOPS = 2 * E * C * H * (K + N)
+
+F32 = mybir.dt.float32
+BF16 = mybir.dt.bfloat16
+U32 = mybir.dt.uint32
+U16 = mybir.dt.uint16
+U8 = mybir.dt.uint8
+FP8X4 = mybir.dt.float8_e4m3fn_x4
+
+P = 128
+PACK = 4
+PASSES = K // (P * PACK)
+PIECES = E * PASSES
+SLOTS = E * C
+HALF = 128
+MULT = mybir.AluOpType.mult
+ADD = mybir.AluOpType.add
+GELU = mybir.ActivationFunctionType.Gelu_apprx_tanh
+
+W1_VECTOR = [0, 0, 0, 84, 84, 84, 84, 84, 84, 84, 84, 84]
+X_VECTOR = [300, 128, 128]
+LAG = 1
+CUTS = [0, 384, 768, 1024]
+
+
+def tile_routed_moe_kernel(tc, xT, w1, w2, gate, offs, pos1, pos2, out):
+    nc = tc.nc
+    with ExitStack() as ctx:
+        keep = ctx.enter_context(tc.tile_pool(name="keep", bufs=1))
+        tokgroups = ctx.enter_context(tc.tile_pool(name="tokgroups", bufs=3))
+        raws = ctx.enter_context(tc.tile_pool(name="raws", bufs=8))
+        groups = ctx.enter_context(tc.tile_pool(name="groups", bufs=5))
+        hidden = ctx.enter_context(tc.tile_pool(name="hidden", bufs=4))
+        psum_h = ctx.enter_context(tc.psum_pool(name="psum_h", bufs=2))
+        psum_t = ctx.enter_context(tc.psum_pool(name="psum_t", bufs=1))
+        psum_y = ctx.enter_context(tc.psum_pool(name="psum_y", bufs=2))
+
+        offs_t = keep.tile([P, SLOTS // 16], U16, name="offs_t")
+        pos1_t = keep.tile([P, T // 16], U16, name="pos1_t")
+        pos2_t = keep.tile([P, T // 16], U16, name="pos2_t")
+
+        xs = keep.tile([P, T], U8, name="xs", align_bytes=64)
+        nc.gpsimd.memset(xs[:], 0)
+
+        x_raw = []
+        w1_raw = {}
+
+        def load_x(g):
+            t = keep.tile([P, PACK, T], F32, name=f"x_raw{g}")
+            src = xT[g * 512 : (g + 1) * 512, :].rearrange("(p j) w -> p j w", j=PACK)
+            if g == 0:
+                nc.sync.dma_start(t[:, :, : T // 2], src[:, :, : T // 2])
+                nc.sync.dma_start(t[:, :, T // 2 :], src[:, :, T // 2 :])
+            else:
+                nc.sync.dma_start(t[:], src)
+            x_raw.append(t)
+
+        def load_w1(q):
+            e, g = q // PASSES, q % PASSES
+            t = raws.tile([P, PACK, H], F32, name="w1_raw")
+            src = w1[e, g * 512 : (g + 1) * 512, :].rearrange("(p j) c -> p j c", j=PACK)
+            if q == PIECES - 1:
+                nc.sync.dma_start(t[:, :, : H // 2], src[:, :, : H // 2])
+                nc.sync.dma_start(t[:, :, H // 2 :], src[:, :, H // 2 :])
+            else:
+                nc.sync.dma_start(t[:], src)
+            w1_raw[q] = t
+
+        w2_raw = keep.tile([P, E, PACK, N], F32, name="w2_raw")
+        gate_t = keep.tile([P, 2, T], F32, name="gate_t")
+        for g in range(PASSES):
+            load_x(g)
+            if g == 0:
+                nc.sync.dma_start(offs_t[:], offs)
+            load_w1(g)
+        nc.sync.dma_start(w2_raw[:], w2.rearrange("e (p j) n -> p e j n", j=PACK))
+        for q in range(PASSES, PIECES):
+            load_w1(q)
+        nc.sync.dma_start(pos1_t[:], pos1)
+        nc.sync.dma_start(pos2_t[:], pos2)
+        nc.sync.dma_start(gate_t[:], gate.rearrange("r n t -> n r t"))
+
+        slot_codes = keep.tile([P, PASSES, SLOTS], U32, name="slot_codes", align_bytes=64)
+        slot_scales = keep.tile([P, SLOTS], U8, name="slot_scales", align_bytes=64)
+        x_codes = []
+
+        def tokens(g):
+            xg = tokgroups.tile([P, T, PACK], BF16, name="xg", align_bytes=64)
+            dst = xg[:].rearrange("p (c i) j -> p c j i", i=4)
+            src = x_raw[g][:].rearrange("p j (c i) -> p c j i", i=4)
+            v = X_VECTOR[g] // 4
+            if g == 0:
+                h = T // 8
+                nc.vector.tensor_copy(dst[:, : v // 2], src[:, : v // 2])
+                nc.scalar.copy(dst[:, v // 2 : h], src[:, v // 2 : h])
+                nc.vector.tensor_copy(dst[:, h : h + v // 2], src[:, h : h + v // 2])
+                nc.scalar.copy(dst[:, h + v // 2 :], src[:, h + v // 2 :])
+            else:
+                nc.vector.tensor_copy(dst[:, :v], src[:, :v])
+                nc.scalar.copy(dst[:, v:], src[:, v:])
+            codes = keep.tile([P, T], U32, name=f"x_codes{g}", align_bytes=64)
+            nc.vector.quantize_mx(
+                out=codes[:].bitcast(FP8X4), scales=xs[4 * g : P, :], in_=xg[:].rearrange("p w j -> p (w j)")
+            )
+            x_codes.append(codes)
+
+        def gather(dst, window, c):
+            a, b = CUTS[c], CUTS[c + 1]
+            nc.vector.tensor_copy(dst[:, a:b], window[:].indirect(offs_t[:, a // 16 : b // 16]))
+
+        w2_codes = keep.tile([P, E * N], U32, name="w2_codes", align_bytes=64)
+        w2_scales = keep.tile([P, E * N], U8, name="w2_scales", align_bytes=64)
+
+        def second_weights():
+            w2g = keep.tile([P, E, N, PACK], BF16, name="w2g", align_bytes=64)
+            for e in range(E):
+                nc.scalar.copy(
+                    w2g[:, e].rearrange("p (c i) j -> p c j i", i=4),
+                    w2_raw[:, e].rearrange("p j (c i) -> p c j i", i=4),
+                )
+            nc.vector.quantize_mx(
+                out=w2_codes[:].bitcast(FP8X4), scales=w2_scales[:], in_=w2g[:].rearrange("p e n j -> p (e n j)")
+            )
+
+        y_all = keep.tile([P, SLOTS], F32, name="y_all")
+        w1_grouped = {}
+        w1_mx = {}
+
+        def interleave(q):
+            wg = groups.tile([P, H * PACK], BF16, name="wg", align_bytes=64)
+            dst = wg[:].rearrange("p (t m j) -> p m j t", t=4, j=PACK)
+            src = w1_raw[q][:].rearrange("p j (m t) -> p m j t", t=4)
+            v = W1_VECTOR[q]
+            if q == PIECES - 1:
+                h = P // 2
+                for m0 in (0, h):
+                    vm = m0 + v // 2
+                    nc.vector.tensor_copy(dst[:, m0:vm], src[:, m0:vm])
+                    nc.scalar.copy(dst[:, vm : m0 + h], src[:, vm : m0 + h])
+            else:
+                if v > 0:
+                    nc.vector.tensor_copy(dst[:, :v], src[:, :v])
+                if v < P:
+                    nc.scalar.copy(dst[:, v:], src[:, v:])
+            w1_grouped[q] = wg
+
+        def quantize(q):
+            codes = keep.tile([P, H], U32, name=f"w1_codes{q}", align_bytes=64)
+            scales = keep.tile([P, H], U8, name=f"w1_scales{q}", align_bytes=64)
+            parts = 4 if q == PIECES - 1 else 1
+            for i in range(parts):
+                cols = slice(i * H // parts, (i + 1) * H // parts)
+                wide = slice(i * H * PACK // parts, (i + 1) * H * PACK // parts)
+                nc.vector.quantize_mx(
+                    out=codes[:, cols].bitcast(FP8X4), scales=scales[:, cols], in_=w1_grouped[q][:, wide]
+                )
+            w1_mx[q] = (codes, scales)
+
+        h_psum = {}
+
+        def first_layer(e):
+            for b in range(C // HALF):
+                cols = slice(e * C + b * HALF, e * C + (b + 1) * HALF)
+                hp = psum_h.tile([P, 4, HALF], F32, name="hp")
+                for t in range(4):
+                    rows = slice(t * P, (t + 1) * P)
+                    for g in range(PASSES):
+                        codes, scales = w1_mx[e * PASSES + g]
+                        nc.tensor.matmul_mx(
+                            out=hp[:, t, :],
+                            lhsT=codes[:, rows].bitcast(FP8X4),
+                            lhsT_scale=scales[:, rows],
+                            rhs=slot_codes[:, g, cols].bitcast(FP8X4),
+                            rhs_scale=slot_scales[4 * g : P, cols],
+                            start=(g == 0),
+                            stop=(g == PASSES - 1),
+                        )
+                h_psum[(e, b)] = hp
+
+        h_grouped = {}
+
+        def activate(e):
+            for b in range(C // HALF):
+                if e + 1 < E:
+                    span = w1_grouped[(e + 1) * PASSES + LAG][:, b * HALF * PACK : (b + 1) * HALF * PACK]
+                else:
+                    hg = hidden.tile([P, HALF * PACK], BF16, name="hg", align_bytes=64)
+                    span = hg[:]
+                nc.scalar.activation(
+                    span.rearrange("p (n j) -> p n j", j=PACK), h_psum[(e, b)][:].rearrange("p t n -> p n t"), GELU
+                )
+                h_grouped[(e, b)] = span
+
+        y_psum = {}
+
+        def second_layer(e):
+            yp = psum_y.tile([P, C], F32, name="yp")
+            for b in range(C // HALF):
+                cols = slice(b * HALF, (b + 1) * HALF)
+                h_codes = hidden.tile([P, HALF], U32, name="h_codes", align_bytes=64)
+                h_scales = hidden.tile([P, HALF], U8, name="h_scales", align_bytes=64)
+                nc.vector.quantize_mx(out=h_codes[:].bitcast(FP8X4), scales=h_scales[:], in_=h_grouped[(e, b)])
+                nc.tensor.matmul_mx(
+                    out=yp[:, cols],
+                    lhsT=w2_codes[:, e * N : (e + 1) * N].bitcast(FP8X4),
+                    lhsT_scale=w2_scales[:, e * N : (e + 1) * N],
+                    rhs=h_codes[:].bitcast(FP8X4),
+                    rhs_scale=h_scales[:],
+                    start=True,
+                    stop=True,
+                )
+            y_psum[e] = yp
+
+        def collect(e):
+            if e + 1 < E:
+                nc.scalar.copy(y_all[:, e * C : (e + 1) * C], y_psum[e][:])
+            else:
+                for b in range(C // HALF):
+                    nc.vector.tensor_copy(
+                        y_all[:, e * C + b * HALF : e * C + (b + 1) * HALF], y_psum[e][:, b * HALF : (b + 1) * HALF]
+                    )
+
+        tail_psum = [psum_t.tile([P, C], F32, name=f"tail{t}") for t in range(4)]
+
+        def tail_pass(g):
+            codes, scales = w1_mx[(E - 1) * PASSES + g]
+            cols = slice((E - 1) * C, SLOTS)
+            for t in range(4):
+                rows = slice(t * P, (t + 1) * P)
+                nc.tensor.matmul_mx(
+                    out=tail_psum[t][:],
+                    lhsT=codes[:, rows].bitcast(FP8X4),
+                    lhsT_scale=scales[:, rows],
+                    rhs=slot_codes[:, g, cols].bitcast(FP8X4),
+                    rhs_scale=slot_scales[4 * g : P, cols],
+                    start=(g == 0),
+                    stop=(g == PASSES - 1),
+                )
+
+        def tail_end():
+            hb = keep.tile([P, 4, C], BF16, name="hb", align_bytes=64)
+            for t in range(4):
+                nc.scalar.activation(hb[:, t, :], tail_psum[t][:], GELU)
+            hg = keep.tile([P, C, PACK], BF16, name="hg", align_bytes=64)
+            nc.vector.tensor_copy(
+                hg[:].rearrange("p (c i) t -> p c t i", i=4), hb[:].rearrange("p t (c i) -> p c t i", i=4)
+            )
+            h_codes = keep.tile([P, C], U32, name="tail_codes", align_bytes=64)
+            h_scales = keep.tile([P, C], U8, name="tail_scales", align_bytes=64)
+            nc.vector.quantize_mx(
+                out=h_codes[:].bitcast(FP8X4), scales=h_scales[:], in_=hg[:].rearrange("p n t -> p (n t)")
+            )
+            yp = psum_y.tile([P, C], F32, name="yp")
+            nc.tensor.matmul_mx(
+                out=yp[:],
+                lhsT=w2_codes[:, (E - 1) * N :].bitcast(FP8X4),
+                lhsT_scale=w2_scales[:, (E - 1) * N :],
+                rhs=h_codes[:].bitcast(FP8X4),
+                rhs_scale=h_scales[:],
+                start=True,
+                stop=True,
+            )
+            nc.vector.tensor_copy(y_all[:, (E - 1) * C :], yp[:])
+
+        for g in range(PASSES):
+            tokens(g)
+        for c in range(len(CUTS) - 1):
+            for g in range(PASSES):
+                gather(slot_codes[:, g, :], x_codes[g], c)
+            gather(slot_scales, xs, c)
+        for q in range(PIECES + 1):
+            if q < PIECES:
+                interleave(q)
+            if q >= 1:
+                quantize(q - 1)
+            if q == 3:
+                second_weights()
+            e, g = q // PASSES, q % PASSES
+            if q > (E - 1) * PASSES:
+                tail_pass(q - 1 - (E - 1) * PASSES)
+            if g == 0 and 0 < e < E:
+                first_layer(e - 1)
+            if q == PIECES:
+                tail_end()
+            if g == LAG + 1 and 0 < e < E:
+                activate(e - 1)
+                second_layer(e - 1)
+                collect(e - 1)
+
+        first = keep.tile([P, T], F32, name="first")
+        nc.vector.tensor_tensor(first[:], y_all[:].indirect(pos1_t[:]), gate_t[:, 0, :], MULT)
+        for b in range(2):
+            toks = slice(b * 256, (b + 1) * 256)
+            second = hidden.tile([P, 256], F32, name="second")
+            nc.vector.tensor_tensor(second[:], y_all[:].indirect(pos2_t[:, b * 16 : (b + 1) * 16]), gate_t[:, 1, toks], MULT)
+            total = hidden.tile([P, 256], F32, name="total")
+            nc.vector.tensor_tensor(total[:], first[:, toks], second[:], ADD)
+            nc.sync.dma_start(out[:, toks], total[:])

@@ -22,9 +22,11 @@ MULT = mybir.AluOpType.mult
 ADD = mybir.AluOpType.add
 GELU = mybir.ActivationFunctionType.Gelu_apprx_tanh
 
-W1_VECTOR = [0, 0, 0, 84, 84, 84, 84, 84, 84, 84, 84, 84]
-X_VECTOR = [300, 128, 128]
-LAG = 1
+W1_VECTOR = [0, 0, 0, 72, 72, 72, 72, 72, 72, 72, 72, 64]
+RAW_SLOTS = 8
+RAW_BYTES = PACK * H * 4
+X_VECTOR = [256, 0, 0]
+PACE = [[5, 6], [6, 7], [11, 11]]
 CUTS = [0, 384, 768, 1024]
 
 
@@ -33,11 +35,10 @@ def tile_routed_moe_kernel(tc, xT, w1, w2, gate, offs, pos1, pos2, out):
     with ExitStack() as ctx:
         keep = ctx.enter_context(tc.tile_pool(name="keep", bufs=1))
         tokgroups = ctx.enter_context(tc.tile_pool(name="tokgroups", bufs=3))
-        raws = ctx.enter_context(tc.tile_pool(name="raws", bufs=8))
+        raws = ctx.enter_context(tc.tile_pool(name="raws", bufs=1))
         groups = ctx.enter_context(tc.tile_pool(name="groups", bufs=5))
         hidden = ctx.enter_context(tc.tile_pool(name="hidden", bufs=4))
-        psum_h = ctx.enter_context(tc.psum_pool(name="psum_h", bufs=2))
-        psum_t = ctx.enter_context(tc.psum_pool(name="psum_t", bufs=1))
+        psum_h = ctx.enter_context(tc.psum_pool(name="psum_h", bufs=6))
         psum_y = ctx.enter_context(tc.psum_pool(name="psum_y", bufs=2))
 
         offs_t = keep.tile([P, SLOTS // 16], U16, name="offs_t")
@@ -62,7 +63,7 @@ def tile_routed_moe_kernel(tc, xT, w1, w2, gate, offs, pos1, pos2, out):
 
         def load_w1(q):
             e, g = q // PASSES, q % PASSES
-            t = raws.tile([P, PACK, H], F32, name="w1_raw")
+            t = raws.tile([P, PACK, H], F32, name=f"w1_raw{q}", offset=q % RAW_SLOTS * RAW_BYTES, align_bytes=64)
             src = w1[e, g * 512 : (g + 1) * 512, :].rearrange("(p j) c -> p j c", j=PACK)
             if q == PIECES - 1:
                 nc.sync.dma_start(t[:, :, : H // 2], src[:, :, : H // 2])
@@ -77,13 +78,12 @@ def tile_routed_moe_kernel(tc, xT, w1, w2, gate, offs, pos1, pos2, out):
             load_x(g)
             if g == 0:
                 nc.sync.dma_start(offs_t[:], offs)
+        w2_rows = w2.rearrange("e (p j) n -> p e j n", j=PACK)
+        for g in range(PASSES):
             load_w1(g)
-        nc.sync.dma_start(w2_raw[:], w2.rearrange("e (p j) n -> p e j n", j=PACK))
-        for q in range(PASSES, PIECES):
+        nc.sync.dma_start(w2_raw[:, : E - 1], w2_rows[:, : E - 1])
+        for q in range(PASSES, RAW_SLOTS):
             load_w1(q)
-        nc.sync.dma_start(pos1_t[:], pos1)
-        nc.sync.dma_start(pos2_t[:], pos2)
-        nc.sync.dma_start(gate_t[:], gate.rearrange("r n t -> n r t"))
 
         slot_codes = keep.tile([P, PASSES, SLOTS], U32, name="slot_codes", align_bytes=64)
         slot_scales = keep.tile([P, SLOTS], U8, name="slot_scales", align_bytes=64)
@@ -101,7 +101,6 @@ def tile_routed_moe_kernel(tc, xT, w1, w2, gate, offs, pos1, pos2, out):
                 nc.vector.tensor_copy(dst[:, h : h + v // 2], src[:, h : h + v // 2])
                 nc.scalar.copy(dst[:, h + v // 2 :], src[:, h + v // 2 :])
             else:
-                nc.vector.tensor_copy(dst[:, :v], src[:, :v])
                 nc.scalar.copy(dst[:, v:], src[:, v:])
             codes = keep.tile([P, T], U32, name=f"x_codes{g}", align_bytes=64)
             nc.vector.quantize_mx(
@@ -116,15 +115,20 @@ def tile_routed_moe_kernel(tc, xT, w1, w2, gate, offs, pos1, pos2, out):
         w2_codes = keep.tile([P, E * N], U32, name="w2_codes", align_bytes=64)
         w2_scales = keep.tile([P, E * N], U8, name="w2_scales", align_bytes=64)
 
-        def second_weights():
-            w2g = keep.tile([P, E, N, PACK], BF16, name="w2g", align_bytes=64)
-            for e in range(E):
-                nc.scalar.copy(
-                    w2g[:, e].rearrange("p (c i) j -> p c j i", i=4),
-                    w2_raw[:, e].rearrange("p j (c i) -> p c j i", i=4),
-                )
+        w2g = keep.tile([P, E, N, PACK], BF16, name="w2g", align_bytes=64)
+
+        def second_weights(e):
+            dst = w2g[:, e].rearrange("p (c i) j -> p c j i", i=4)
+            src = w2_raw[:, e].rearrange("p j (c i) -> p c j i", i=4)
+            if e + 1 < E:
+                nc.scalar.copy(dst, src)
+            else:
+                nc.vector.tensor_copy(dst, src)
+            cols = slice(e * N, (e + 1) * N)
             nc.vector.quantize_mx(
-                out=w2_codes[:].bitcast(FP8X4), scales=w2_scales[:], in_=w2g[:].rearrange("p e n j -> p (e n j)")
+                out=w2_codes[:, cols].bitcast(FP8X4),
+                scales=w2_scales[:, cols],
+                in_=w2g[:, e].rearrange("p n j -> p (n j)"),
             )
 
         y_all = keep.tile([P, SLOTS], F32, name="y_all")
@@ -182,39 +186,33 @@ def tile_routed_moe_kernel(tc, xT, w1, w2, gate, offs, pos1, pos2, out):
                         )
                 h_psum[(e, b)] = hp
 
-        h_grouped = {}
-
-        def activate(e):
-            for b in range(C // HALF):
-                if e + 1 < E:
-                    span = w1_grouped[(e + 1) * PASSES + LAG][:, b * HALF * PACK : (b + 1) * HALF * PACK]
-                else:
-                    hg = hidden.tile([P, HALF * PACK], BF16, name="hg", align_bytes=64)
-                    span = hg[:]
-                nc.scalar.activation(
-                    span.rearrange("p (n j) -> p n j", j=PACK), h_psum[(e, b)][:].rearrange("p t n -> p n t"), GELU
-                )
-                h_grouped[(e, b)] = span
-
         y_psum = {}
 
-        def second_layer(e):
-            yp = psum_y.tile([P, C], F32, name="yp")
-            for b in range(C // HALF):
-                cols = slice(b * HALF, (b + 1) * HALF)
-                h_codes = hidden.tile([P, HALF], U32, name="h_codes", align_bytes=64)
-                h_scales = hidden.tile([P, HALF], U8, name="h_scales", align_bytes=64)
-                nc.vector.quantize_mx(out=h_codes[:].bitcast(FP8X4), scales=h_scales[:], in_=h_grouped[(e, b)])
-                nc.tensor.matmul_mx(
-                    out=yp[:, cols],
-                    lhsT=w2_codes[:, e * N : (e + 1) * N].bitcast(FP8X4),
-                    lhsT_scale=w2_scales[:, e * N : (e + 1) * N],
-                    rhs=h_codes[:].bitcast(FP8X4),
-                    rhs_scale=h_scales[:],
-                    start=True,
-                    stop=True,
-                )
-            y_psum[e] = yp
+        def second_layer(e, b):
+            if e + 1 < E:
+                place = PACE[e][b] % RAW_SLOTS * RAW_BYTES + b * HALF * PACK * 2
+                hg = raws.tile([P, HALF * PACK], BF16, name=f"hg{e}_{b}", offset=place, align_bytes=64)
+            else:
+                hg = hidden.tile([P, HALF * PACK], BF16, name="hg", align_bytes=64)
+            span = hg[:]
+            nc.scalar.activation(
+                span.rearrange("p (n j) -> p n j", j=PACK), h_psum[(e, b)][:].rearrange("p t n -> p n t"), GELU
+            )
+            if b == 0:
+                yp = psum_y.tile([P, C], F32, name="yp")
+                y_psum[e] = yp
+            h_codes = hidden.tile([P, HALF], U32, name="h_codes", align_bytes=64)
+            h_scales = hidden.tile([P, HALF], U8, name="h_scales", align_bytes=64)
+            nc.vector.quantize_mx(out=h_codes[:].bitcast(FP8X4), scales=h_scales[:], in_=span)
+            nc.tensor.matmul_mx(
+                out=y_psum[e][:, b * HALF : (b + 1) * HALF],
+                lhsT=w2_codes[:, e * N : (e + 1) * N].bitcast(FP8X4),
+                lhsT_scale=w2_scales[:, e * N : (e + 1) * N],
+                rhs=h_codes[:].bitcast(FP8X4),
+                rhs_scale=h_scales[:],
+                start=True,
+                stop=True,
+            )
 
         def collect(e):
             if e + 1 < E:
@@ -225,48 +223,6 @@ def tile_routed_moe_kernel(tc, xT, w1, w2, gate, offs, pos1, pos2, out):
                         y_all[:, e * C + b * HALF : e * C + (b + 1) * HALF], y_psum[e][:, b * HALF : (b + 1) * HALF]
                     )
 
-        tail_psum = [psum_t.tile([P, C], F32, name=f"tail{t}") for t in range(4)]
-
-        def tail_pass(g):
-            codes, scales = w1_mx[(E - 1) * PASSES + g]
-            cols = slice((E - 1) * C, SLOTS)
-            for t in range(4):
-                rows = slice(t * P, (t + 1) * P)
-                nc.tensor.matmul_mx(
-                    out=tail_psum[t][:],
-                    lhsT=codes[:, rows].bitcast(FP8X4),
-                    lhsT_scale=scales[:, rows],
-                    rhs=slot_codes[:, g, cols].bitcast(FP8X4),
-                    rhs_scale=slot_scales[4 * g : P, cols],
-                    start=(g == 0),
-                    stop=(g == PASSES - 1),
-                )
-
-        def tail_end():
-            hb = keep.tile([P, 4, C], BF16, name="hb", align_bytes=64)
-            for t in range(4):
-                nc.scalar.activation(hb[:, t, :], tail_psum[t][:], GELU)
-            hg = keep.tile([P, C, PACK], BF16, name="hg", align_bytes=64)
-            nc.vector.tensor_copy(
-                hg[:].rearrange("p (c i) t -> p c t i", i=4), hb[:].rearrange("p t (c i) -> p c t i", i=4)
-            )
-            h_codes = keep.tile([P, C], U32, name="tail_codes", align_bytes=64)
-            h_scales = keep.tile([P, C], U8, name="tail_scales", align_bytes=64)
-            nc.vector.quantize_mx(
-                out=h_codes[:].bitcast(FP8X4), scales=h_scales[:], in_=hg[:].rearrange("p n t -> p (n t)")
-            )
-            yp = psum_y.tile([P, C], F32, name="yp")
-            nc.tensor.matmul_mx(
-                out=yp[:],
-                lhsT=w2_codes[:, (E - 1) * N :].bitcast(FP8X4),
-                lhsT_scale=w2_scales[:, (E - 1) * N :],
-                rhs=h_codes[:].bitcast(FP8X4),
-                rhs_scale=h_scales[:],
-                start=True,
-                stop=True,
-            )
-            nc.vector.tensor_copy(y_all[:, (E - 1) * C :], yp[:])
-
         for g in range(PASSES):
             tokens(g)
         for c in range(len(CUTS) - 1):
@@ -276,21 +232,29 @@ def tile_routed_moe_kernel(tc, xT, w1, w2, gate, offs, pos1, pos2, out):
         for q in range(PIECES + 1):
             if q < PIECES:
                 interleave(q)
+            if q + RAW_SLOTS < PIECES:
+                load_w1(q + RAW_SLOTS)
+            elif q + RAW_SLOTS == PIECES:
+                nc.sync.dma_start(w2_raw[:, E - 1], w2_rows[:, E - 1])
+                nc.sync.dma_start(pos1_t[:], pos1)
+                nc.sync.dma_start(pos2_t[:], pos2)
+                nc.sync.dma_start(gate_t[:], gate.rearrange("r n t -> n r t"))
             if q >= 1:
                 quantize(q - 1)
             if q == 3:
-                second_weights()
-            e, g = q // PASSES, q % PASSES
-            if q > (E - 1) * PASSES:
-                tail_pass(q - 1 - (E - 1) * PASSES)
-            if g == 0 and 0 < e < E:
-                first_layer(e - 1)
+                for e in range(E - 1):
+                    second_weights(e)
             if q == PIECES:
-                tail_end()
-            if g == LAG + 1 and 0 < e < E:
-                activate(e - 1)
-                second_layer(e - 1)
-                collect(e - 1)
+                second_weights(E - 1)
+            e, g = q // PASSES, q % PASSES
+            if g == 0 and e > 0:
+                first_layer(e - 1)
+            for d in range(E):
+                for b in range(C // HALF):
+                    if q == (PACE[d][b] + 1 if d + 1 < E else PIECES):
+                        second_layer(d, b)
+                        if b == 1:
+                            collect(d)
 
         first = keep.tile([P, T], F32, name="first")
         nc.vector.tensor_tensor(first[:], y_all[:].indirect(pos1_t[:]), gate_t[:, 0, :], MULT)

@@ -12,256 +12,251 @@ U16 = mybir.dt.uint16
 U8 = mybir.dt.uint8
 FP8X4 = mybir.dt.float8_e4m3fn_x4
 
-P = 128
-PACK = 4
-PASSES = K // (P * PACK)
-PIECES = E * PASSES
-SLOTS = E * C
-HALF = 128
 MULT = mybir.AluOpType.mult
 ADD = mybir.AluOpType.add
 GELU = mybir.ActivationFunctionType.Gelu_apprx_tanh
 
-W1_VECTOR = [0, 0, 0, 72, 72, 72, 72, 72, 72, 72, 72, 64]
-RAW_SLOTS = 8
+P = 128
+PACK = 4
+K_PASS = P * PACK
+PASSES = K // K_PASS
+PIECES = E * PASSES
+SLOTS = E * C
+HALF = C // 2
+TILES = H // P
+LINE = 4
+LIST_ROWS = 16
+
+SCALE_ROWS = 4
+SLOT_CUTS = [0, 384, 768, 1024]
+LATE_EXPERTS = 2
+
+VECTOR_TOKENS = [256, 128, 128]
+VECTOR_GROUPS = [0, 0, 0, 72, 64, 64, 72, 128, 128, 64, 72, 72]
+
+RAW_PLACES = 8
 RAW_BYTES = PACK * H * 4
-X_VECTOR = [256, 0, 0]
-PACE = [[5, 6], [6, 7], [11, 11]]
-CUTS = [0, 384, 768, 1024]
+GELU_OVER = [[5, 6], [6, 7], [11, 11]]
+LAST_PARTS = 4
+
+
+def place_of(q):
+    return q % RAW_PLACES * RAW_BYTES
+
+
+def shared_copy(nc, dst, src, cut):
+    if cut > 0:
+        nc.vector.tensor_copy(dst[:, :cut], src[:, :cut])
+    if cut < dst.shape[1]:
+        nc.scalar.copy(dst[:, cut:], src[:, cut:])
 
 
 def tile_routed_moe_kernel(tc, xT, w1, w2, gate, offs, pos1, pos2, out):
     nc = tc.nc
     with ExitStack() as ctx:
         keep = ctx.enter_context(tc.tile_pool(name="keep", bufs=1))
-        tokgroups = ctx.enter_context(tc.tile_pool(name="tokgroups", bufs=3))
+        token_groups = ctx.enter_context(tc.tile_pool(name="token_groups", bufs=PASSES))
         raws = ctx.enter_context(tc.tile_pool(name="raws", bufs=1))
-        groups = ctx.enter_context(tc.tile_pool(name="groups", bufs=5))
+        w1_groups = ctx.enter_context(tc.tile_pool(name="w1_groups", bufs=5))
         hidden = ctx.enter_context(tc.tile_pool(name="hidden", bufs=4))
         psum_h = ctx.enter_context(tc.psum_pool(name="psum_h", bufs=6))
         psum_y = ctx.enter_context(tc.psum_pool(name="psum_y", bufs=2))
 
-        offs_t = keep.tile([P, SLOTS // 16], U16, name="offs_t")
-        pos1_t = keep.tile([P, T // 16], U16, name="pos1_t")
-        pos2_t = keep.tile([P, T // 16], U16, name="pos2_t")
+        offs_list = keep.tile([P, SLOTS // LIST_ROWS], U16, name="offs_list")
+        pos1_list = keep.tile([P, T // LIST_ROWS], U16, name="pos1_list")
+        pos2_list = keep.tile([P, T // LIST_ROWS], U16, name="pos2_list")
+        gate_rows = keep.tile([P, 2, T], F32, name="gate_rows")
 
-        xs = keep.tile([P, T], U8, name="xs", align_bytes=64)
-        nc.gpsimd.memset(xs[:], 0)
+        token_scales = keep.tile([P, T], U8, name="token_scales", align_bytes=64)
+        nc.gpsimd.memset(token_scales[:], 0)
 
         x_raw = []
-        w1_raw = {}
-
-        def load_x(g):
-            t = keep.tile([P, PACK, T], F32, name=f"x_raw{g}")
-            src = xT[g * 512 : (g + 1) * 512, :].rearrange("(p j) w -> p j w", j=PACK)
+        for g in range(PASSES):
+            raw = keep.tile([P, PACK, T], F32, name=f"x_raw{g}")
+            nc.sync.dma_start(raw[:], xT[g * K_PASS : (g + 1) * K_PASS, :].rearrange("(p j) t -> p j t", j=PACK))
+            x_raw.append(raw)
             if g == 0:
-                nc.sync.dma_start(t[:, :, : T // 2], src[:, :, : T // 2])
-                nc.sync.dma_start(t[:, :, T // 2 :], src[:, :, T // 2 :])
-            else:
-                nc.sync.dma_start(t[:], src)
-            x_raw.append(t)
+                nc.sync.dma_start(offs_list[:], offs)
+
+        w1_raw = {}
 
         def load_w1(q):
             e, g = q // PASSES, q % PASSES
-            t = raws.tile([P, PACK, H], F32, name=f"w1_raw{q}", offset=q % RAW_SLOTS * RAW_BYTES, align_bytes=64)
-            src = w1[e, g * 512 : (g + 1) * 512, :].rearrange("(p j) c -> p j c", j=PACK)
-            if q == PIECES - 1:
-                nc.sync.dma_start(t[:, :, : H // 2], src[:, :, : H // 2])
-                nc.sync.dma_start(t[:, :, H // 2 :], src[:, :, H // 2 :])
-            else:
-                nc.sync.dma_start(t[:], src)
-            w1_raw[q] = t
+            raw = raws.tile([P, PACK, H], F32, name=f"w1_raw{q}", offset=place_of(q), align_bytes=64)
+            src = w1[e, g * K_PASS : (g + 1) * K_PASS, :].rearrange("(p j) c -> p j c", j=PACK)
+            halves = 2 if q == PIECES - 1 else 1
+            for i in range(halves):
+                rows = slice(i * PACK // halves, (i + 1) * PACK // halves)
+                nc.sync.dma_start(raw[:, rows], src[:, rows])
+            w1_raw[q] = raw
 
         w2_raw = keep.tile([P, E, PACK, N], F32, name="w2_raw")
-        gate_t = keep.tile([P, 2, T], F32, name="gate_t")
-        for g in range(PASSES):
-            load_x(g)
-            if g == 0:
-                nc.sync.dma_start(offs_t[:], offs)
         w2_rows = w2.rearrange("e (p j) n -> p e j n", j=PACK)
-        for g in range(PASSES):
-            load_w1(g)
-        nc.sync.dma_start(w2_raw[:, : E - 1], w2_rows[:, : E - 1])
-        for q in range(PASSES, RAW_SLOTS):
+
+        for q in range(PASSES):
             load_w1(q)
+        nc.sync.dma_start(w2_raw[:, : E - LATE_EXPERTS], w2_rows[:, : E - LATE_EXPERTS])
+        for q in range(PASSES, RAW_PLACES):
+            load_w1(q)
+
+        token_codes = []
+        for g in range(PASSES):
+            grouped = token_groups.tile([P, T, PACK], BF16, name="grouped", align_bytes=64)
+            shared_copy(
+                nc,
+                grouped[:].rearrange("p (c i) j -> p c j i", i=LINE),
+                x_raw[g][:].rearrange("p j (c i) -> p c j i", i=LINE),
+                VECTOR_TOKENS[g] // LINE,
+            )
+            codes = keep.tile([P, T], U32, name=f"token_codes{g}", align_bytes=64)
+            nc.vector.quantize_mx(
+                out=codes[:].bitcast(FP8X4),
+                scales=token_scales[SCALE_ROWS * g : P, :],
+                in_=grouped[:].rearrange("p t j -> p (t j)"),
+            )
+            token_codes.append(codes)
 
         slot_codes = keep.tile([P, PASSES, SLOTS], U32, name="slot_codes", align_bytes=64)
         slot_scales = keep.tile([P, SLOTS], U8, name="slot_scales", align_bytes=64)
-        x_codes = []
+        for a, b in zip(SLOT_CUTS[:-1], SLOT_CUTS[1:]):
+            entries = offs_list[:, a // LIST_ROWS : b // LIST_ROWS]
+            for g in range(PASSES):
+                nc.vector.tensor_copy(slot_codes[:, g, a:b], token_codes[g][:].indirect(entries))
+            nc.vector.tensor_copy(slot_scales[:, a:b], token_scales[:].indirect(entries))
 
-        def tokens(g):
-            xg = tokgroups.tile([P, T, PACK], BF16, name="xg", align_bytes=64)
-            dst = xg[:].rearrange("p (c i) j -> p c j i", i=4)
-            src = x_raw[g][:].rearrange("p j (c i) -> p c j i", i=4)
-            v = X_VECTOR[g] // 4
-            if g == 0:
-                h = T // 8
-                nc.vector.tensor_copy(dst[:, : v // 2], src[:, : v // 2])
-                nc.scalar.copy(dst[:, v // 2 : h], src[:, v // 2 : h])
-                nc.vector.tensor_copy(dst[:, h : h + v // 2], src[:, h : h + v // 2])
-                nc.scalar.copy(dst[:, h + v // 2 :], src[:, h + v // 2 :])
-            else:
-                nc.scalar.copy(dst[:, v:], src[:, v:])
-            codes = keep.tile([P, T], U32, name=f"x_codes{g}", align_bytes=64)
-            nc.vector.quantize_mx(
-                out=codes[:].bitcast(FP8X4), scales=xs[4 * g : P, :], in_=xg[:].rearrange("p w j -> p (w j)")
-            )
-            x_codes.append(codes)
+        w1_grouped = {}
+        w1_codes = {}
+        w1_scales = {}
 
-        def gather(dst, window, c):
-            a, b = CUTS[c], CUTS[c + 1]
-            nc.vector.tensor_copy(dst[:, a:b], window[:].indirect(offs_t[:, a // 16 : b // 16]))
+        def interleave(q):
+            grouped = w1_groups.tile([P, H * PACK], BF16, name="w1_grouped", align_bytes=64)
+            dst = grouped[:].rearrange("p (t m j) -> p m j t", t=TILES, j=PACK)
+            src = w1_raw[q][:].rearrange("p j (m t) -> p m j t", t=TILES)
+            halves = 2 if q == PIECES - 1 else 1
+            for i in range(halves):
+                rows = slice(i * PACK // halves, (i + 1) * PACK // halves)
+                shared_copy(nc, dst[:, :, rows], src[:, :, rows], VECTOR_GROUPS[q])
+            w1_grouped[q] = grouped
 
+        def quantise(q):
+            codes = keep.tile([P, H], U32, name=f"w1_codes{q}", align_bytes=64)
+            scales = keep.tile([P, H], U8, name=f"w1_scales{q}", align_bytes=64)
+            parts = LAST_PARTS if q == PIECES - 1 else 1
+            width = H // parts
+            for i in range(parts):
+                cols = slice(i * width, (i + 1) * width)
+                nc.vector.quantize_mx(
+                    out=codes[:, cols].bitcast(FP8X4),
+                    scales=scales[:, cols],
+                    in_=w1_grouped[q][:, i * width * PACK : (i + 1) * width * PACK],
+                )
+            w1_codes[q] = codes
+            w1_scales[q] = scales
+
+        w2_grouped = keep.tile([P, E, N, PACK], BF16, name="w2_grouped", align_bytes=64)
         w2_codes = keep.tile([P, E * N], U32, name="w2_codes", align_bytes=64)
         w2_scales = keep.tile([P, E * N], U8, name="w2_scales", align_bytes=64)
 
-        w2g = keep.tile([P, E, N, PACK], BF16, name="w2g", align_bytes=64)
-
-        def second_weights(e):
-            dst = w2g[:, e].rearrange("p (c i) j -> p c j i", i=4)
-            src = w2_raw[:, e].rearrange("p j (c i) -> p c j i", i=4)
-            if e + 1 < E:
-                nc.scalar.copy(dst, src)
-            else:
-                nc.vector.tensor_copy(dst, src)
-            cols = slice(e * N, (e + 1) * N)
+        def second_weights(first, last, copy):
+            for e in range(first, last):
+                copy(
+                    w2_grouped[:, e].rearrange("p (c i) j -> p c j i", i=LINE),
+                    w2_raw[:, e].rearrange("p j (c i) -> p c j i", i=LINE),
+                )
+            cols = slice(first * N, last * N)
             nc.vector.quantize_mx(
                 out=w2_codes[:, cols].bitcast(FP8X4),
                 scales=w2_scales[:, cols],
-                in_=w2g[:, e].rearrange("p n j -> p (n j)"),
+                in_=w2_grouped[:, first:last].rearrange("p e n j -> p (e n j)"),
             )
 
-        y_all = keep.tile([P, SLOTS], F32, name="y_all")
-        w1_grouped = {}
-        w1_mx = {}
-
-        def interleave(q):
-            wg = groups.tile([P, H * PACK], BF16, name="wg", align_bytes=64)
-            dst = wg[:].rearrange("p (t m j) -> p m j t", t=4, j=PACK)
-            src = w1_raw[q][:].rearrange("p j (m t) -> p m j t", t=4)
-            v = W1_VECTOR[q]
-            if q == PIECES - 1:
-                h = P // 2
-                for m0 in (0, h):
-                    vm = m0 + v // 2
-                    nc.vector.tensor_copy(dst[:, m0:vm], src[:, m0:vm])
-                    nc.scalar.copy(dst[:, vm : m0 + h], src[:, vm : m0 + h])
-            else:
-                if v > 0:
-                    nc.vector.tensor_copy(dst[:, :v], src[:, :v])
-                if v < P:
-                    nc.scalar.copy(dst[:, v:], src[:, v:])
-            w1_grouped[q] = wg
-
-        def quantize(q):
-            codes = keep.tile([P, H], U32, name=f"w1_codes{q}", align_bytes=64)
-            scales = keep.tile([P, H], U8, name=f"w1_scales{q}", align_bytes=64)
-            parts = 4 if q == PIECES - 1 else 1
-            for i in range(parts):
-                cols = slice(i * H // parts, (i + 1) * H // parts)
-                wide = slice(i * H * PACK // parts, (i + 1) * H * PACK // parts)
-                nc.vector.quantize_mx(
-                    out=codes[:, cols].bitcast(FP8X4), scales=scales[:, cols], in_=w1_grouped[q][:, wide]
-                )
-            w1_mx[q] = (codes, scales)
-
-        h_psum = {}
+        hidden_sums = {}
 
         def first_layer(e):
-            for b in range(C // HALF):
+            for b in range(2):
                 cols = slice(e * C + b * HALF, e * C + (b + 1) * HALF)
-                hp = psum_h.tile([P, 4, HALF], F32, name="hp")
-                for t in range(4):
-                    rows = slice(t * P, (t + 1) * P)
+                sums = psum_h.tile([P, TILES, HALF], F32, name="hidden_sums")
+                for t in range(TILES):
+                    channels = slice(t * P, (t + 1) * P)
                     for g in range(PASSES):
-                        codes, scales = w1_mx[e * PASSES + g]
+                        q = e * PASSES + g
                         nc.tensor.matmul_mx(
-                            out=hp[:, t, :],
-                            lhsT=codes[:, rows].bitcast(FP8X4),
-                            lhsT_scale=scales[:, rows],
+                            out=sums[:, t, :],
+                            lhsT=w1_codes[q][:, channels].bitcast(FP8X4),
+                            lhsT_scale=w1_scales[q][:, channels],
                             rhs=slot_codes[:, g, cols].bitcast(FP8X4),
-                            rhs_scale=slot_scales[4 * g : P, cols],
+                            rhs_scale=slot_scales[SCALE_ROWS * g : P, cols],
                             start=(g == 0),
                             stop=(g == PASSES - 1),
                         )
-                h_psum[(e, b)] = hp
+                hidden_sums[(e, b)] = sums
 
-        y_psum = {}
+        y_sums = {}
 
         def second_layer(e, b):
-            if e + 1 < E:
-                place = PACE[e][b] % RAW_SLOTS * RAW_BYTES + b * HALF * PACK * 2
-                hg = raws.tile([P, HALF * PACK], BF16, name=f"hg{e}_{b}", offset=place, align_bytes=64)
+            if e < E - 1:
+                place = place_of(GELU_OVER[e][b]) + b * HALF * PACK * 2
+                h = raws.tile([P, HALF * PACK], BF16, name=f"h{e}_{b}", offset=place, align_bytes=64)
             else:
-                hg = hidden.tile([P, HALF * PACK], BF16, name="hg", align_bytes=64)
-            span = hg[:]
+                h = hidden.tile([P, HALF * PACK], BF16, name="h_last", align_bytes=64)
             nc.scalar.activation(
-                span.rearrange("p (n j) -> p n j", j=PACK), h_psum[(e, b)][:].rearrange("p t n -> p n t"), GELU
+                h[:].rearrange("p (s t) -> p s t", t=TILES), hidden_sums[(e, b)][:].rearrange("p t s -> p s t"), GELU
             )
+            codes = hidden.tile([P, HALF], U32, name="h_codes", align_bytes=64)
+            scales = hidden.tile([P, HALF], U8, name="h_scales", align_bytes=64)
+            nc.vector.quantize_mx(out=codes[:].bitcast(FP8X4), scales=scales[:], in_=h[:])
             if b == 0:
-                yp = psum_y.tile([P, C], F32, name="yp")
-                y_psum[e] = yp
-            h_codes = hidden.tile([P, HALF], U32, name="h_codes", align_bytes=64)
-            h_scales = hidden.tile([P, HALF], U8, name="h_scales", align_bytes=64)
-            nc.vector.quantize_mx(out=h_codes[:].bitcast(FP8X4), scales=h_scales[:], in_=span)
+                sums = psum_y.tile([P, C], F32, name="y_sums")
+                y_sums[e] = sums
+            channels = slice(e * N, (e + 1) * N)
             nc.tensor.matmul_mx(
-                out=y_psum[e][:, b * HALF : (b + 1) * HALF],
-                lhsT=w2_codes[:, e * N : (e + 1) * N].bitcast(FP8X4),
-                lhsT_scale=w2_scales[:, e * N : (e + 1) * N],
-                rhs=h_codes[:].bitcast(FP8X4),
-                rhs_scale=h_scales[:],
+                out=y_sums[e][:, b * HALF : (b + 1) * HALF],
+                lhsT=w2_codes[:, channels].bitcast(FP8X4),
+                lhsT_scale=w2_scales[:, channels],
+                rhs=codes[:].bitcast(FP8X4),
+                rhs_scale=scales[:],
                 start=True,
                 stop=True,
             )
 
-        def collect(e):
-            if e + 1 < E:
-                nc.scalar.copy(y_all[:, e * C : (e + 1) * C], y_psum[e][:])
-            else:
-                for b in range(C // HALF):
-                    nc.vector.tensor_copy(
-                        y_all[:, e * C + b * HALF : e * C + (b + 1) * HALF], y_psum[e][:, b * HALF : (b + 1) * HALF]
-                    )
+        y_slots = keep.tile([P, SLOTS], F32, name="y_slots")
 
-        for g in range(PASSES):
-            tokens(g)
-        for c in range(len(CUTS) - 1):
-            for g in range(PASSES):
-                gather(slot_codes[:, g, :], x_codes[g], c)
-            gather(slot_scales, xs, c)
-        for q in range(PIECES + 1):
-            if q < PIECES:
-                interleave(q)
-            if q + RAW_SLOTS < PIECES:
-                load_w1(q + RAW_SLOTS)
-            elif q + RAW_SLOTS == PIECES:
-                nc.sync.dma_start(w2_raw[:, E - 1], w2_rows[:, E - 1])
-                nc.sync.dma_start(pos1_t[:], pos1)
-                nc.sync.dma_start(pos2_t[:], pos2)
-                nc.sync.dma_start(gate_t[:], gate.rearrange("r n t -> n r t"))
-            if q >= 1:
-                quantize(q - 1)
-            if q == 3:
-                for e in range(E - 1):
-                    second_weights(e)
-            if q == PIECES:
-                second_weights(E - 1)
-            e, g = q // PASSES, q % PASSES
-            if g == 0 and e > 0:
-                first_layer(e - 1)
-            for d in range(E):
-                for b in range(C // HALF):
-                    if q == (PACE[d][b] + 1 if d + 1 < E else PIECES):
-                        second_layer(d, b)
+        for q in range(PIECES):
+            interleave(q)
+            if q + RAW_PLACES < PIECES:
+                load_w1(q + RAW_PLACES)
+            elif q + RAW_PLACES == PIECES:
+                nc.sync.dma_start(w2_raw[:, E - LATE_EXPERTS :], w2_rows[:, E - LATE_EXPERTS :])
+                nc.sync.dma_start(pos1_list[:], pos1)
+                nc.sync.dma_start(pos2_list[:], pos2)
+                nc.sync.dma_start(gate_rows[:], gate.rearrange("r n t -> n r t"))
+            quantise(q)
+            if q == PASSES - 1:
+                second_weights(0, E - LATE_EXPERTS, nc.scalar.copy)
+            if q == PIECES - 1:
+                second_weights(E - LATE_EXPERTS, E, nc.vector.tensor_copy)
+            if q % PASSES == PASSES - 1:
+                first_layer(q // PASSES)
+            for e in range(E - 1):
+                for b in range(2):
+                    if q == GELU_OVER[e][b]:
+                        second_layer(e, b)
                         if b == 1:
-                            collect(d)
+                            nc.scalar.copy(y_slots[:, e * C : (e + 1) * C], y_sums[e][:])
+        for b in range(2):
+            second_layer(E - 1, b)
+        for b in range(2):
+            cols = slice((E - 1) * C + b * HALF, (E - 1) * C + (b + 1) * HALF)
+            nc.vector.tensor_copy(y_slots[:, cols], y_sums[E - 1][:, b * HALF : (b + 1) * HALF])
 
         first = keep.tile([P, T], F32, name="first")
-        nc.vector.tensor_tensor(first[:], y_all[:].indirect(pos1_t[:]), gate_t[:, 0, :], MULT)
-        for b in range(2):
-            toks = slice(b * 256, (b + 1) * 256)
-            second = hidden.tile([P, 256], F32, name="second")
-            nc.vector.tensor_tensor(second[:], y_all[:].indirect(pos2_t[:, b * 16 : (b + 1) * 16]), gate_t[:, 1, toks], MULT)
-            total = hidden.tile([P, 256], F32, name="total")
-            nc.vector.tensor_tensor(total[:], first[:, toks], second[:], ADD)
-            nc.sync.dma_start(out[:, toks], total[:])
+        nc.vector.tensor_tensor(first[:], y_slots[:].indirect(pos1_list[:]), gate_rows[:, 0, :], MULT)
+        width = T // 2
+        for i in range(2):
+            tokens = slice(i * width, (i + 1) * width)
+            entries = pos2_list[:, i * width // LIST_ROWS : (i + 1) * width // LIST_ROWS]
+            second = hidden.tile([P, width], F32, name="second")
+            nc.vector.tensor_tensor(second[:], y_slots[:].indirect(entries), gate_rows[:, 1, tokens], MULT)
+            total = hidden.tile([P, width], F32, name="total")
+            nc.vector.tensor_tensor(total[:], first[:, tokens], second[:], ADD)
+            nc.sync.dma_start(out[:, tokens], total[:])

@@ -31,8 +31,8 @@ SCALE_ROWS = 4
 SLOT_CUTS = [0, 384, 768, 1024]
 LATE_EXPERTS = 2
 
-VECTOR_TOKENS = [256, 128, 128]
-VECTOR_GROUPS = [0, 0, 0, 72, 64, 64, 72, 128, 128, 64, 72, 72]
+VECTOR_TOKENS = [256, 64, 64]
+VECTOR_GROUPS = [0, 0, 0, 72, 72, 72, 72, 96, 96, 72, 72, 80]
 
 RAW_PLACES = 8
 RAW_BYTES = PACK * H * 4
@@ -59,8 +59,8 @@ def tile_routed_moe_kernel(tc, xT, w1, w2, gate, offs, pos1, pos2, out):
         raws = ctx.enter_context(tc.tile_pool(name="raws", bufs=1))
         w1_groups = ctx.enter_context(tc.tile_pool(name="w1_groups", bufs=5))
         hidden = ctx.enter_context(tc.tile_pool(name="hidden", bufs=4))
-        psum_h = ctx.enter_context(tc.psum_pool(name="psum_h", bufs=6))
-        psum_y = ctx.enter_context(tc.psum_pool(name="psum_y", bufs=2))
+        psum_h = ctx.enter_context(tc.psum_pool(name="psum_h", bufs=5))
+        psum_y = ctx.enter_context(tc.psum_pool(name="psum_y", bufs=3))
 
         offs_list = keep.tile([P, SLOTS // LIST_ROWS], U16, name="offs_list")
         pos1_list = keep.tile([P, T // LIST_ROWS], U16, name="pos1_list")
@@ -84,10 +84,7 @@ def tile_routed_moe_kernel(tc, xT, w1, w2, gate, offs, pos1, pos2, out):
             e, g = q // PASSES, q % PASSES
             raw = raws.tile([P, PACK, H], F32, name=f"w1_raw{q}", offset=place_of(q), align_bytes=64)
             src = w1[e, g * K_PASS : (g + 1) * K_PASS, :].rearrange("(p j) c -> p j c", j=PACK)
-            halves = 2 if q == PIECES - 1 else 1
-            for i in range(halves):
-                rows = slice(i * PACK // halves, (i + 1) * PACK // halves)
-                nc.sync.dma_start(raw[:, rows], src[:, rows])
+            nc.sync.dma_start(raw[:], src)
             w1_raw[q] = raw
 
         w2_raw = keep.tile([P, E, PACK, N], F32, name="w2_raw")
@@ -132,10 +129,7 @@ def tile_routed_moe_kernel(tc, xT, w1, w2, gate, offs, pos1, pos2, out):
             grouped = w1_groups.tile([P, H * PACK], BF16, name="w1_grouped", align_bytes=64)
             dst = grouped[:].rearrange("p (t m j) -> p m j t", t=TILES, j=PACK)
             src = w1_raw[q][:].rearrange("p j (m t) -> p m j t", t=TILES)
-            halves = 2 if q == PIECES - 1 else 1
-            for i in range(halves):
-                rows = slice(i * PACK // halves, (i + 1) * PACK // halves)
-                shared_copy(nc, dst[:, :, rows], src[:, :, rows], VECTOR_GROUPS[q])
+            shared_copy(nc, dst, src, VECTOR_GROUPS[q])
             w1_grouped[q] = grouped
 
         def quantise(q):
@@ -205,12 +199,14 @@ def tile_routed_moe_kernel(tc, xT, w1, w2, gate, offs, pos1, pos2, out):
             codes = hidden.tile([P, HALF], U32, name="h_codes", align_bytes=64)
             scales = hidden.tile([P, HALF], U8, name="h_scales", align_bytes=64)
             nc.vector.quantize_mx(out=codes[:].bitcast(FP8X4), scales=scales[:], in_=h[:])
-            if b == 0:
+            if b == 0 or e == E - 1:
                 sums = psum_y.tile([P, C], F32, name="y_sums")
-                y_sums[e] = sums
+                y_sums[(e, b)] = sums
+            else:
+                y_sums[(e, b)] = y_sums[(e, 0)]
             channels = slice(e * N, (e + 1) * N)
             nc.tensor.matmul_mx(
-                out=y_sums[e][:, b * HALF : (b + 1) * HALF],
+                out=y_sums[(e, b)][:, b * HALF : (b + 1) * HALF],
                 lhsT=w2_codes[:, channels].bitcast(FP8X4),
                 lhsT_scale=w2_scales[:, channels],
                 rhs=codes[:].bitcast(FP8X4),
@@ -242,21 +238,22 @@ def tile_routed_moe_kernel(tc, xT, w1, w2, gate, offs, pos1, pos2, out):
                     if q == GELU_OVER[e][b]:
                         second_layer(e, b)
                         if b == 1:
-                            nc.scalar.copy(y_slots[:, e * C : (e + 1) * C], y_sums[e][:])
+                            nc.scalar.copy(y_slots[:, e * C : (e + 1) * C], y_sums[(e, 0)][:])
         for b in range(2):
             second_layer(E - 1, b)
-        for b in range(2):
+        for b, copy in ((0, nc.vector.tensor_copy), (1, nc.scalar.copy)):
             cols = slice((E - 1) * C + b * HALF, (E - 1) * C + (b + 1) * HALF)
-            nc.vector.tensor_copy(y_slots[:, cols], y_sums[E - 1][:, b * HALF : (b + 1) * HALF])
+            copy(y_slots[:, cols], y_sums[(E - 1, b)][:, b * HALF : (b + 1) * HALF])
 
         first = keep.tile([P, T], F32, name="first")
         nc.vector.tensor_tensor(first[:], y_slots[:].indirect(pos1_list[:]), gate_rows[:, 0, :], MULT)
         width = T // 2
-        for i in range(2):
-            tokens = slice(i * width, (i + 1) * width)
-            entries = pos2_list[:, i * width // LIST_ROWS : (i + 1) * width // LIST_ROWS]
-            second = hidden.tile([P, width], F32, name="second")
-            nc.vector.tensor_tensor(second[:], y_slots[:].indirect(entries), gate_rows[:, 1, tokens], MULT)
+        token_halves = [slice(i * width, (i + 1) * width) for i in range(2)]
+        second = keep.tile([P, T], F32, name="second")
+        for tokens in token_halves:
+            entries = pos2_list[:, tokens.start // LIST_ROWS : tokens.stop // LIST_ROWS]
+            nc.vector.tensor_tensor(second[:, tokens], y_slots[:].indirect(entries), gate_rows[:, 1, tokens], MULT)
+        for tokens in token_halves:
             total = hidden.tile([P, width], F32, name="total")
-            nc.vector.tensor_tensor(total[:], first[:, tokens], second[:], ADD)
+            nc.vector.tensor_tensor(total[:], first[:, tokens], second[:, tokens], ADD)
             nc.sync.dma_start(out[:, tokens], total[:])

from contextlib import ExitStack

import concourse.mybir as mybir

K, T, E, C, H, N = 1536, 512, 4, 256, 512, 128
FLOPS = 2 * E * C * H * (K + N)

F32 = mybir.dt.float32
BF16 = mybir.dt.bfloat16
U32 = mybir.dt.uint32
U16 = mybir.dt.uint16
U8 = mybir.dt.uint8
FP8X4 = mybir.dt.float8_e4m3fn_x4

MULT = mybir.AluOpType.mult
ADD = mybir.AluOpType.add
GELU = mybir.ActivationFunctionType.Gelu_apprx_tanh

P = 128
PACK = 4
K_PASS = P * PACK
PASSES = K // K_PASS
PIECES = E * PASSES
SLOTS = E * C
HALF = C // 2
TILES = H // P
LINE = 4
LIST_ROWS = 16

SCALE_ROWS = 4
SLOT_CUTS = [0, 384, 768, 1024]
LATE_EXPERTS = 2

VECTOR_TOKENS = [256, 64, 64]
VECTOR_GROUPS = [0, 0, 0, 72, 72, 72, 72, 96, 96, 72, 72, 80]

RAW_PLACES = 8
RAW_BYTES = PACK * H * 4
GELU_OVER = [[5, 6], [6, 7], [11, 11]]
LAST_PARTS = 4


def place_of(q):
    return q % RAW_PLACES * RAW_BYTES


def shared_copy(nc, dst, src, cut):
    if cut > 0:
        nc.vector.tensor_copy(dst[:, :cut], src[:, :cut])
    if cut < dst.shape[1]:
        nc.scalar.copy(dst[:, cut:], src[:, cut:])


def tile_routed_moe_kernel(tc, xT, w1, w2, gate, offs, pos1, pos2, out):
    nc = tc.nc
    with ExitStack() as ctx:
        keep = ctx.enter_context(tc.tile_pool(name="keep", bufs=1))
        token_groups = ctx.enter_context(tc.tile_pool(name="token_groups", bufs=PASSES))
        raws = ctx.enter_context(tc.tile_pool(name="raws", bufs=1))
        w1_groups = ctx.enter_context(tc.tile_pool(name="w1_groups", bufs=5))
        hidden = ctx.enter_context(tc.tile_pool(name="hidden", bufs=4))
        psum_h = ctx.enter_context(tc.psum_pool(name="psum_h", bufs=5))
        psum_y = ctx.enter_context(tc.psum_pool(name="psum_y", bufs=3))

        offs_list = keep.tile([P, SLOTS // LIST_ROWS], U16, name="offs_list")
        pos1_list = keep.tile([P, T // LIST_ROWS], U16, name="pos1_list")
        pos2_list = keep.tile([P, T // LIST_ROWS], U16, name="pos2_list")
        gate_rows = keep.tile([P, 2, T], F32, name="gate_rows")

        token_scales = keep.tile([P, T], U8, name="token_scales", align_bytes=64)
        nc.gpsimd.memset(token_scales[:], 0)

        x_raw = []
        for g in range(PASSES):
            raw = keep.tile([P, PACK, T], F32, name=f"x_raw{g}")
            nc.sync.dma_start(raw[:], xT[g * K_PASS : (g + 1) * K_PASS, :].rearrange("(p j) t -> p j t", j=PACK))
            x_raw.append(raw)
            if g == 0:
                nc.sync.dma_start(offs_list[:], offs)

        w1_raw = {}

        def load_w1(q):
            e, g = q // PASSES, q % PASSES
            raw = raws.tile([P, PACK, H], F32, name=f"w1_raw{q}", offset=place_of(q), align_bytes=64)
            src = w1[e, g * K_PASS : (g + 1) * K_PASS, :].rearrange("(p j) c -> p j c", j=PACK)
            nc.sync.dma_start(raw[:], src)
            w1_raw[q] = raw

        w2_raw = keep.tile([P, E, PACK, N], F32, name="w2_raw")
        w2_rows = w2.rearrange("e (p j) n -> p e j n", j=PACK)

        for q in range(PASSES):
            load_w1(q)
        nc.sync.dma_start(w2_raw[:, : E - LATE_EXPERTS], w2_rows[:, : E - LATE_EXPERTS])
        for q in range(PASSES, RAW_PLACES):
            load_w1(q)

        token_codes = []
        for g in range(PASSES):
            grouped = token_groups.tile([P, T, PACK], BF16, name="grouped", align_bytes=64)
            shared_copy(
                nc,
                grouped[:].rearrange("p (c i) j -> p c j i", i=LINE),
                x_raw[g][:].rearrange("p j (c i) -> p c j i", i=LINE),
                VECTOR_TOKENS[g] // LINE,
            )
            codes = keep.tile([P, T], U32, name=f"token_codes{g}", align_bytes=64)
            nc.vector.quantize_mx(
                out=codes[:].bitcast(FP8X4),
                scales=token_scales[SCALE_ROWS * g : P, :],
                in_=grouped[:].rearrange("p t j -> p (t j)"),
            )
            token_codes.append(codes)

        slot_codes = keep.tile([P, PASSES, SLOTS], U32, name="slot_codes", align_bytes=64)
        slot_scales = keep.tile([P, SLOTS], U8, name="slot_scales", align_bytes=64)
        for a, b in zip(SLOT_CUTS[:-1], SLOT_CUTS[1:]):
            entries = offs_list[:, a // LIST_ROWS : b // LIST_ROWS]
            for g in range(PASSES):
                nc.vector.tensor_copy(slot_codes[:, g, a:b], token_codes[g][:].indirect(entries))
            nc.vector.tensor_copy(slot_scales[:, a:b], token_scales[:].indirect(entries))

        w1_grouped = {}
        w1_codes = {}
        w1_scales = {}

        def interleave(q):
            grouped = w1_groups.tile([P, H * PACK], BF16, name="w1_grouped", align_bytes=64)
            dst = grouped[:].rearrange("p (t m j) -> p m j t", t=TILES, j=PACK)
            src = w1_raw[q][:].rearrange("p j (m t) -> p m j t", t=TILES)
            shared_copy(nc, dst, src, VECTOR_GROUPS[q])
            w1_grouped[q] = grouped

        def quantise(q):
            codes = keep.tile([P, H], U32, name=f"w1_codes{q}", align_bytes=64)
            scales = keep.tile([P, H], U8, name=f"w1_scales{q}", align_bytes=64)
            parts = LAST_PARTS if q == PIECES - 1 else 1
            width = H // parts
            for i in range(parts):
                cols = slice(i * width, (i + 1) * width)
                nc.vector.quantize_mx(
                    out=codes[:, cols].bitcast(FP8X4),
                    scales=scales[:, cols],
                    in_=w1_grouped[q][:, i * width * PACK : (i + 1) * width * PACK],
                )
            w1_codes[q] = codes
            w1_scales[q] = scales

        w2_grouped = keep.tile([P, E, N, PACK], BF16, name="w2_grouped", align_bytes=64)
        w2_codes = keep.tile([P, E * N], U32, name="w2_codes", align_bytes=64)
        w2_scales = keep.tile([P, E * N], U8, name="w2_scales", align_bytes=64)

        def second_weights(first, last, copy):
            for e in range(first, last):
                copy(
                    w2_grouped[:, e].rearrange("p (c i) j -> p c j i", i=LINE),
                    w2_raw[:, e].rearrange("p j (c i) -> p c j i", i=LINE),
                )
            cols = slice(first * N, last * N)
            nc.vector.quantize_mx(
                out=w2_codes[:, cols].bitcast(FP8X4),
                scales=w2_scales[:, cols],
                in_=w2_grouped[:, first:last].rearrange("p e n j -> p (e n j)"),
            )

        hidden_sums = {}

        def first_layer(e):
            for b in range(2):
                cols = slice(e * C + b * HALF, e * C + (b + 1) * HALF)
                sums = psum_h.tile([P, TILES, HALF], F32, name="hidden_sums")
                for t in range(TILES):
                    channels = slice(t * P, (t + 1) * P)
                    for g in range(PASSES):
                        q = e * PASSES + g
                        nc.tensor.matmul_mx(
                            out=sums[:, t, :],
                            lhsT=w1_codes[q][:, channels].bitcast(FP8X4),
                            lhsT_scale=w1_scales[q][:, channels],
                            rhs=slot_codes[:, g, cols].bitcast(FP8X4),
                            rhs_scale=slot_scales[SCALE_ROWS * g : P, cols],
                            start=(g == 0),
                            stop=(g == PASSES - 1),
                        )
                hidden_sums[(e, b)] = sums

        y_sums = {}

        def second_layer(e, b):
            if e < E - 1:
                place = place_of(GELU_OVER[e][b]) + b * HALF * PACK * 2
                h = raws.tile([P, HALF * PACK], BF16, name=f"h{e}_{b}", offset=place, align_bytes=64)
            else:
                h = hidden.tile([P, HALF * PACK], BF16, name="h_last", align_bytes=64)
            nc.scalar.activation(
                h[:].rearrange("p (s t) -> p s t", t=TILES), hidden_sums[(e, b)][:].rearrange("p t s -> p s t"), GELU
            )
            codes = hidden.tile([P, HALF], U32, name="h_codes", align_bytes=64)
            scales = hidden.tile([P, HALF], U8, name="h_scales", align_bytes=64)
            nc.vector.quantize_mx(out=codes[:].bitcast(FP8X4), scales=scales[:], in_=h[:])
            if b == 0 or e == E - 1:
                sums = psum_y.tile([P, C], F32, name="y_sums")
                y_sums[(e, b)] = sums
            else:
                y_sums[(e, b)] = y_sums[(e, 0)]
            channels = slice(e * N, (e + 1) * N)
            nc.tensor.matmul_mx(
                out=y_sums[(e, b)][:, b * HALF : (b + 1) * HALF],
                lhsT=w2_codes[:, channels].bitcast(FP8X4),
                lhsT_scale=w2_scales[:, channels],
                rhs=codes[:].bitcast(FP8X4),
                rhs_scale=scales[:],
                start=True,
                stop=True,
            )

        y_slots = keep.tile([P, SLOTS], F32, name="y_slots")

        for q in range(PIECES):
            interleave(q)
            if q + RAW_PLACES < PIECES:
                load_w1(q + RAW_PLACES)
            elif q + RAW_PLACES == PIECES:
                nc.sync.dma_start(w2_raw[:, E - LATE_EXPERTS :], w2_rows[:, E - LATE_EXPERTS :])
                nc.sync.dma_start(pos1_list[:], pos1)
                nc.sync.dma_start(pos2_list[:], pos2)
                nc.sync.dma_start(gate_rows[:], gate.rearrange("r n t -> n r t"))
            quantise(q)
            if q == PASSES - 1:
                second_weights(0, E - LATE_EXPERTS, nc.scalar.copy)
            if q == PIECES - 1:
                second_weights(E - LATE_EXPERTS, E, nc.vector.tensor_copy)
            if q % PASSES == PASSES - 1:
                first_layer(q // PASSES)
            for e in range(E - 1):
                for b in range(2):
                    if q == GELU_OVER[e][b]:
                        second_layer(e, b)
                        if b == 1:
                            nc.scalar.copy(y_slots[:, e * C : (e + 1) * C], y_sums[(e, 0)][:])
        for b in range(2):
            second_layer(E - 1, b)
        for b, copy in ((0, nc.vector.tensor_copy), (1, nc.scalar.copy)):
            cols = slice((E - 1) * C + b * HALF, (E - 1) * C + (b + 1) * HALF)
            copy(y_slots[:, cols], y_sums[(E - 1, b)][:, b * HALF : (b + 1) * HALF])

        first = keep.tile([P, T], F32, name="first")
        nc.vector.tensor_tensor(first[:], y_slots[:].indirect(pos1_list[:]), gate_rows[:, 0, :], MULT)
        width = T // 2
        token_halves = [slice(i * width, (i + 1) * width) for i in range(2)]
        second = keep.tile([P, T], F32, name="second")
        for tokens in token_halves:
            entries = pos2_list[:, tokens.start // LIST_ROWS : tokens.stop // LIST_ROWS]
            nc.vector.tensor_tensor(second[:, tokens], y_slots[:].indirect(entries), gate_rows[:, 1, tokens], MULT)
        for tokens in token_halves:
            total = hidden.tile([P, width], F32, name="total")
            nc.vector.tensor_tensor(total[:], first[:, tokens], second[:, tokens], ADD)
            nc.sync.dma_start(out[:, tokens], total[:])
